import numpy as np
import ml_dtypes


def mxq(x, axis, fmt="e4m3"):
    dtype, down = {"e4m3": (ml_dtypes.float8_e4m3fn, 7), "e5m2": (ml_dtypes.float8_e5m2, 14)}[fmt]
    v = np.moveaxis(np.asarray(x, np.float32).astype(ml_dtypes.bfloat16).astype(np.float64), axis, -1)
    blocks = v.reshape(v.shape[:-1] + (-1, 32))
    amax = np.abs(blocks).max(-1, keepdims=True)
    byte = np.maximum(np.where(amax > 0, np.frexp(amax)[1] - 1 + 127, 0) - down, 1)
    scale = np.exp2(byte - 127.0)
    codes = (blocks / scale).astype(np.float32).astype(dtype).astype(np.float64)
    return np.moveaxis((codes * scale).reshape(v.shape), -1, axis)


WIDE = False


def mx_kscale(k):
    if not WIDE:
        return np.ones(k)
    levels = np.array([10, -10, 5, -5, 0])
    if k % 512:
        return np.exp2(np.random.permutation(np.resize(levels, k // 32))).repeat(32)
    a = np.empty((k // 512, 16))
    for p in range(k // 512):
        a[p, :8] = np.random.permutation(np.resize(levels, 8))
        for g in range(8):
            far = levels[np.abs(levels - a[p, g]) >= 10]
            a[p, g + 8] = far[np.random.randint(len(far))]
    return np.exp2(a.ravel()).repeat(32)


def f64(x):
    return np.asarray(x).astype(np.float64)


E2M1 = np.array([0.0, 0.5, 1.0, 1.5, 2.0, 3.0, 4.0, 6.0, -0.0, -0.5, -1.0, -1.5, -2.0, -3.0, -4.0, -6.0])


def pack_weight(w, fmt):
    k, n = w.shape
    w = f64(np.asarray(w, np.float32).astype(ml_dtypes.bfloat16)).reshape(k // 32, 32, n)
    amax = np.abs(w).max(1)
    if fmt == "e4m3":
        byte = np.frexp(amax)[1] - 1 + 127 - 7
    else:
        mant, ex = np.frexp(amax / 6.0)
        byte = np.where(mant > 0.5, ex, ex - 1) + 127
    byte = np.clip(np.where(amax > 0, byte, 1), 1, 254)
    scaled = (w * np.exp2(127.0 - byte)[:, None, :]).reshape(k, n).astype(np.float32)
    by_word = np.ascontiguousarray(scaled.reshape(k // 512, 128, 4, n).transpose(0, 1, 3, 2))
    if fmt == "e4m3":
        words = by_word.astype(ml_dtypes.float8_e4m3fn).view(np.uint8)
    else:
        c = by_word.astype(ml_dtypes.float4_e2m1fn).view(np.uint8) & 0xF
        words = (c[..., 0::2] | (c[..., 1::2] << 4)).reshape(k // 512, 128, 2 * n)
    return np.ascontiguousarray(words), np.ascontiguousarray(byte.astype(np.uint8).reshape(k // 512, 16, n))


def unpack_weight(words, scales, fmt):
    g, _, n = scales.shape
    words = np.ascontiguousarray(words).reshape(g, 128, n, -1)
    if fmt == "e4m3":
        vals = words.view(ml_dtypes.float8_e4m3fn).astype(np.float64)
    else:
        nib = np.empty((g, 128, n, 4), np.uint8)
        nib[..., 0::2] = words & 0xF
        nib[..., 1::2] = words >> 4
        vals = E2M1[nib]
    vals = vals * np.repeat(np.exp2(scales.astype(np.float64) - 127.0), 8, axis=1)[..., None]
    return vals.transpose(0, 1, 3, 2).reshape(g * 512, n)


K, L, T, R, N = 1024, 512, 512, 512, 512


def setup_inputs():
    n = np.random.standard_normal
    fk = mx_kscale(K)
    fl = mx_kscale(L)
    fr = mx_kscale(R)
    xtp = pack_weight(n((K, T)) / fk[:, None], "e4m3")
    wap = pack_weight(n((K, R)) * np.random.uniform(0.3, 2.0, (1, R)) / np.sqrt(K) * fk[:, None], "e2m1")
    xqp = pack_weight(n((L, T)) / fl[:, None], "e4m3")
    wcp = pack_weight(n((L, R)) * 1 / np.sqrt(L) * fl[:, None], "e2m1")
    wbp = pack_weight(n((R, N)) * 1 / np.sqrt(R) / fr[:, None], "e4m3")
    wyp = pack_weight(n((K, N)) * 1 / np.sqrt(K) * fk[:, None], "e2m1")
    return {
        "xt_words": xtp[0],
        "xt_scales": xtp[1],
        "wa_words": wap[0],
        "wa_scales": wap[1],
        "xq_words": xqp[0],
        "xq_scales": xqp[1],
        "wc_words": wcp[0],
        "wc_scales": wcp[1],
        "us": (np.random.uniform(0.5, 2.0, (R, 1)) * fr[:, None]).astype(np.float32),
        "wb_words": wbp[0],
        "wb_scales": wbp[1],
        "wy_words": wyp[0],
        "wy_scales": wyp[1],
    }


def reference(xt_words, xt_scales, wa_words, wa_scales, xq_words, xq_scales, wc_words, wc_scales, us, wb_words, wb_scales, wy_words, wy_scales):
    xtu = unpack_weight(xt_words, xt_scales, "e4m3")
    wau = unpack_weight(wa_words, wa_scales, "e2m1")
    xqu = unpack_weight(xq_words, xq_scales, "e4m3")
    wcu = unpack_weight(wc_words, wc_scales, "e2m1")
    wbu = unpack_weight(wb_words, wb_scales, "e4m3")
    wyu = unpack_weight(wy_words, wy_scales, "e2m1")
    z = wau.T @ xtu + wcu.T @ xqu
    hid = z / (np.max(np.abs(z), axis=1, keepdims=True) + 0.1) * f64(us)
    hidq = mxq(hid, 0, "e4m3")
    y = wbu.T @ hidq + wyu.T @ xtu
    return y

@@ -1,0 +1,247 @@
+from contextlib import ExitStack
+
+import concourse.mybir as mybir
+
+K, L, T, R, N = 1024, 512, 512, 512, 512
+FLOPS = 2 * T * (K * R + L * R + R * N + K * N)
+
+F32 = mybir.dt.float32
+BF16 = mybir.dt.bfloat16
+I32 = mybir.dt.int32
+U32 = mybir.dt.uint32
+U16 = mybir.dt.uint16
+U8 = mybir.dt.uint8
+FP8X4 = mybir.dt.float8_e4m3fn_x4
+FP4X4 = mybir.dt.float4_e2m1fn_x4
+ALU = mybir.AluOpType
+ACT = mybir.ActivationFunctionType
+AXIS = mybir.AxisListType
+
+P = 128
+PACK = 4
+CH = 128
+TENTH = 0.1
+
+
+def tile_mix_hidden_over_its_peak_kernel(
+    tc, xt_words, xt_scales, wa_words, wa_scales, xq_words, xq_scales, wc_words, wc_scales,
+    us, wb_words, wb_scales, wy_words, wy_scales, out,
+):
+    nc = tc.nc
+    with ExitStack() as ctx:
+        sb = ctx.enter_context(tc.tile_pool(name="sb", bufs=1))
+        ps = ctx.enter_context(tc.psum_pool(name="ps", bufs=1))
+        ctx.enter_context(tc.manual_schedule())
+
+        def sbuf(name, shape, dtype):
+            return sb.tile(shape, dtype, name=name, align_bytes=64)
+
+        def plane(name, passes):
+            t = sbuf(name, [P, passes, 512], U8)
+            nc.vector.memset(t[:].bitcast(I32), 0)
+            return t
+
+        def load_scale_rows(queue, dst, src, r):
+            queue.dma_start(
+                out=dst[r:P:32, :, :].bitcast(I32),
+                in_=src.rearrange("g (q r) c -> r q g c", r=4)[r].bitcast(I32),
+            )
+
+        def load_fp8(queue, name, src):
+            t = sbuf(name, [P, src.shape[0], 512], U32)
+            queue.dma_start(out=t[:].bitcast(I32), in_=src.rearrange("g p n t -> p g (n t)").bitcast(I32))
+            return t
+
+        def load_fp4(queue, name, src):
+            t = sbuf(name, [P, src.shape[0], 1024], U8)
+            queue.dma_start(out=t[:].bitcast(I32), in_=src.rearrange("g p b -> p g b").bitcast(I32))
+            return t
+
+        wa_s = plane("wa_s", 2)
+        xt_s = plane("xt_s", 2)
+        xq_s = plane("xq_s", 1)
+        wc_s = plane("wc_s", 1)
+        wy_s = plane("wy_s", 2)
+        wb_s = plane("wb_s", 1)
+
+        wa_w = load_fp4(nc.sync, "wa_w", wa_words)
+        xt_w = load_fp8(nc.scalar, "xt_w", xt_words)
+        for r in range(4):
+            load_scale_rows(nc.sync, wa_s, wa_scales, r)
+        for r in range(2):
+            load_scale_rows(nc.scalar, xt_s, xt_scales, r)
+        for r in range(2, 4):
+            load_scale_rows(nc.gpsimd, xt_s, xt_scales, r)
+        load_scale_rows(nc.gpsimd, xq_s, xq_scales, 0)
+        wc_w = load_fp4(nc.sync, "wc_w", wc_words)
+        for r in range(4):
+            load_scale_rows(nc.sync, wc_s, wc_scales, r)
+        xq_w = load_fp8(nc.sync, "xq_w", xq_words)
+        for r in range(1, 4):
+            load_scale_rows(nc.sync, xq_s, xq_scales, r)
+        us_t = sbuf("us_t", [P, PACK], F32)
+        nc.sync.dma_start(out=us_t[:], in_=us.rearrange("(p j) o -> p (j o)", j=PACK))
+        wy_w = load_fp4(nc.sync, "wy_w", wy_words)
+        for r in range(4):
+            load_scale_rows(nc.sync, wy_s, wy_scales, r)
+        wb_w = load_fp8(nc.sync, "wb_w", wb_words)
+        for r in range(4):
+            load_scale_rows(nc.sync, wb_s, wb_scales, r)
+
+        passes = [
+            (wa_w[:, 0, :], wa_s[:, 0, :], xt_w[:, 0, :], xt_s[:, 0, :]),
+            (wa_w[:, 1, :], wa_s[:, 1, :], xt_w[:, 1, :], xt_s[:, 1, :]),
+            (wc_w[:, 0, :], wc_s[:, 0, :], xq_w[:, 0, :], xq_s[:, 0, :]),
+        ]
+        w1, s1 = [], []
+        for g in range(3):
+            wp = sbuf("w1_%d" % g, [P, 1024], U8)
+            sp = sbuf("s1_%d" % g, [P, 512], U8)
+            nc.vector.tensor_copy(
+                out=wp[:].bitcast(U16).rearrange("p (j m) -> p j m", j=PACK),
+                in_=passes[g][0].bitcast(U16).rearrange("p (m j) -> p j m", j=PACK),
+            )
+            nc.vector.tensor_copy(
+                out=sp[:].rearrange("p (j m) -> p j m", j=PACK),
+                in_=passes[g][1].rearrange("p (m j) -> p j m", j=PACK),
+            )
+            w1.append(wp)
+            s1.append(sp)
+
+        inv_us = sbuf("inv_us", [P, PACK - 1], F32)
+        nc.vector.reciprocal(out=inv_us[:], in_=us_t[:, 0 : PACK - 1])
+
+        def z_pass(dst, j, g, t0, width, start, stop):
+            nc.tensor.matmul_mx(
+                out=dst,
+                lhsT=w1[g][:, 256 * j : 256 * (j + 1)].bitcast(FP4X4),
+                lhsT_scale=s1[g][:, P * j : P * (j + 1)],
+                rhs=passes[g][2][:, t0 : t0 + width].bitcast(FP8X4),
+                rhs_scale=passes[g][3][:, t0 : t0 + width],
+                start=start,
+                stop=stop,
+            )
+
+        zb = [ps.tile([P, T], F32, name="z%d" % j, tag="bank%d" % j) for j in range(3)]
+        zl = [ps.tile([P, T // 2], F32, name="zl%d" % h, tag="bank%d" % (3 + h)) for h in range(2)]
+        for g in range(3):
+            for j in range(2):
+                z_pass(zb[j][:], j, g, 0, T, g == 0, g == 2)
+        for g in range(3):
+            z_pass(zb[2][:], 2, g, 0, T, g == 0, g == 2)
+        for h in range(2):
+            for g in range(3):
+                for c in range(2):
+                    z_pass(zl[h][:, CH * c : CH * (c + 1)], 3, g, 256 * h + CH * c, CH,
+                           g == 0 and c == 0, g == 2 and c == 1)
+
+        zs = sbuf("zs", [P, PACK, T], F32)
+        peak = sbuf("peak", [P, PACK - 1], F32)
+        denom = sbuf("denom", [P, PACK], F32)
+        part = sbuf("part", [P, 1], F32)
+        gain = sbuf("gain", [P, PACK], F32)
+        mag = [sbuf("mag%d" % h, [P, T // 2], F32) for h in range(2)]
+        for j in range(3):
+            nc.scalar.activation(out=zs[:, j, :], in_=zb[j][:], func=ACT.Copy)
+            nc.vector.tensor_reduce(
+                out=peak[:, j : j + 1], in_=zs[:, j, :], axis=AXIS.X, op=ALU.max, apply_absolute_value=True
+            )
+        for h in range(2):
+            nc.scalar.activation(out=mag[h][:], in_=zl[h][:], func=ACT.Abs)
+        for h in range(2):
+            nc.scalar.activation(
+                out=zs[:, 3, 256 * h : 256 * (h + 1)], in_=zl[h][:], func=ACT.Copy, scale=us_t[:, 3:4]
+            )
+        nc.vector.tensor_scalar(
+            out=mag[0][:], in0=mag[0][:], scalar1=TENTH, scalar2=None, op0=ALU.add, op1=ALU.max, accum_out=part[:]
+        )
+        nc.vector.scalar_tensor_tensor(
+            out=denom[:, 0:3], in0=peak[:], scalar=TENTH, in1=inv_us[:], op0=ALU.add, op1=ALU.mult
+        )
+        nc.vector.tensor_scalar(
+            out=mag[1][:], in0=mag[1][:], scalar1=TENTH, scalar2=part[:], op0=ALU.add, op1=ALU.max,
+            accum_out=denom[:, 3:4],
+        )
+        nc.vector.reciprocal(out=gain[:], in_=denom[:])
+
+        chunks = T // CH
+        hb = [sbuf("hb%d" % c, [P, CH * PACK], BF16) for c in range(chunks)]
+        hq = [sbuf("hq%d" % c, [P, CH], U32) for c in range(chunks)]
+        hs = [sbuf("hs%d" % c, [P, CH], U8) for c in range(chunks)]
+
+        def scale_tokens(c, a, b):
+            u = (b - a) // 2
+            nc.vector.tensor_tensor(
+                out=hb[c][:, PACK * a : PACK * b].rearrange("p (u i j) -> p u j i", i=2, j=PACK),
+                in0=zs[:, :, CH * c + a : CH * c + b].rearrange("p j (u i) -> p u j i", i=2),
+                in1=gain[:].rearrange("p (a j b) -> p a j b", a=1, b=1).broadcast_to([P, u, PACK, 2]),
+                op=ALU.mult,
+            )
+
+        def quantize(c):
+            nc.vector.quantize_mx(out=hq[c][:].bitcast(FP8X4), scales=hs[c][:], in_=hb[c][:])
+
+        banks = [(0, 0, 4, 5), (1, 0, 4, 6), (2, 0, 4, 7), (3, 0, 2, 0), (3, 2, 2, 1)]
+        yb = {}
+
+        def skip(b):
+            c, n0, nn, bank = banks[b]
+            yb[b] = ps.tile([P, nn, CH], F32, name="y%d" % b, tag="bank%d" % bank)
+            for i in range(nn):
+                for g in range(2):
+                    n = n0 + i
+                    nc.tensor.matmul_mx(
+                        out=yb[b][:, i, :],
+                        lhsT=wy_w[:, g, 256 * n : 256 * (n + 1)].bitcast(FP4X4),
+                        lhsT_scale=wy_s[:, g, P * n : P * (n + 1)],
+                        rhs=xt_w[:, g, CH * c : CH * (c + 1)].bitcast(FP8X4),
+                        rhs_scale=xt_s[:, g, CH * c : CH * (c + 1)],
+                        start=(i == 0 and g == 0),
+                        stop=False,
+                    )
+
+        def second(b):
+            c, n0, nn, bank = banks[b]
+            for i in range(nn):
+                n = n0 + i
+                nc.tensor.matmul_mx(
+                    out=yb[b][:, i, :],
+                    lhsT=wb_w[:, 0, P * n : P * (n + 1)].bitcast(FP8X4),
+                    lhsT_scale=wb_s[:, 0, P * n : P * (n + 1)],
+                    rhs=hq[c][:].bitcast(FP8X4),
+                    rhs_scale=hs[c][:],
+                    start=False,
+                    stop=(i == nn - 1),
+                )
+
+        out_v = out.rearrange("(i p) t -> p i t", p=P)
+
+        def drain(b, on_vector):
+            c, n0, nn, bank = banks[b]
+            res = sbuf("res%d" % b, [P, nn, CH], F32)
+            if on_vector:
+                nc.vector.tensor_copy(out=res[:], in_=yb[b][:])
+            else:
+                nc.scalar.copy(out=res[:], in_=yb[b][:])
+            nc.sync.dma_start(out=out_v[:, n0 : n0 + nn, CH * c : CH * (c + 1)], in_=res[:])
+
+        skip(0)
+        skip(1)
+        skip(2)
+        scale_tokens(0, 0, CH)
+        for c in range(chunks):
+            if c + 1 < chunks:
+                scale_tokens(c + 1, 0, CH // 2)
+            quantize(c)
+            if c + 1 < chunks:
+                scale_tokens(c + 1, CH // 2, CH)
+            if c < 3:
+                second(c)
+                drain(c, False)
+            if c == 0:
+                skip(3)
+                skip(4)
+        second(3)
+        second(4)
+        drain(3, False)
+        drain(4, True)

@@ -20,7 +20,9 @@ AXIS = mybir.AxisListType
 P = 128
 PACK = 4
 CH = 128
+HALF = T // 2
 TENTH = 0.1
+SCALAR_TOKENS = 96
 
 
 def tile_mix_hidden_over_its_peak_kernel(
@@ -58,26 +60,26 @@ def tile_mix_hidden_over_its_peak_kernel(
             return t
 
         wa_s = plane("wa_s", 2)
+        wc_s = plane("wc_s", 1)
         xt_s = plane("xt_s", 2)
         xq_s = plane("xq_s", 1)
-        wc_s = plane("wc_s", 1)
         wy_s = plane("wy_s", 2)
         wb_s = plane("wb_s", 1)
 
+        queues = [nc.sync, nc.scalar]
         wa_w = load_fp4(nc.sync, "wa_w", wa_words)
+        for r in range(4):
+            load_scale_rows(queues[(r + 1) % 2], wa_s, wa_scales, r)
+        wc_w = load_fp4(nc.scalar, "wc_w", wc_words)
+        load_scale_rows(nc.sync, wc_s, wc_scales, 0)
         xt_w = load_fp8(nc.scalar, "xt_w", xt_words)
+        load_scale_rows(nc.gpsimd, wc_s, wc_scales, 3)
         for r in range(4):
-            load_scale_rows(nc.sync, wa_s, wa_scales, r)
-        for r in range(2):
-            load_scale_rows(nc.scalar, xt_s, xt_scales, r)
-        for r in range(2, 4):
-            load_scale_rows(nc.gpsimd, xt_s, xt_scales, r)
-        load_scale_rows(nc.gpsimd, xq_s, xq_scales, 0)
-        wc_w = load_fp4(nc.sync, "wc_w", wc_words)
-        for r in range(4):
-            load_scale_rows(nc.sync, wc_s, wc_scales, r)
+            load_scale_rows(queues[r % 2], xt_s, xt_scales, r)
         xq_w = load_fp8(nc.sync, "xq_w", xq_words)
-        for r in range(1, 4):
+        for r in range(1, 3):
+            load_scale_rows(queues[r % 2], wc_s, wc_scales, r)
+        for r in range(4):
             load_scale_rows(nc.sync, xq_s, xq_scales, r)
         us_t = sbuf("us_t", [P, PACK], F32)
         nc.sync.dma_start(out=us_t[:], in_=us.rearrange("(p j) o -> p (j o)", j=PACK))
@@ -93,20 +95,17 @@ def tile_mix_hidden_over_its_peak_kernel(
             (wa_w[:, 1, :], wa_s[:, 1, :], xt_w[:, 1, :], xt_s[:, 1, :]),
             (wc_w[:, 0, :], wc_s[:, 0, :], xq_w[:, 0, :], xq_s[:, 0, :]),
         ]
-        w1, s1 = [], []
+        w1 = [sbuf("w1_%d" % g, [P, 1024], U8) for g in range(3)]
+        s1 = [sbuf("s1_%d" % g, [P, 512], U8) for g in range(3)]
         for g in range(3):
-            wp = sbuf("w1_%d" % g, [P, 1024], U8)
-            sp = sbuf("s1_%d" % g, [P, 512], U8)
             nc.vector.tensor_copy(
-                out=wp[:].bitcast(U16).rearrange("p (j m) -> p j m", j=PACK),
+                out=w1[g][:].bitcast(U16).rearrange("p (j m) -> p j m", j=PACK),
                 in_=passes[g][0].bitcast(U16).rearrange("p (m j) -> p j m", j=PACK),
             )
             nc.vector.tensor_copy(
-                out=sp[:].rearrange("p (j m) -> p j m", j=PACK),
+                out=s1[g][:].rearrange("p (j m) -> p j m", j=PACK),
                 in_=passes[g][1].rearrange("p (m j) -> p j m", j=PACK),
             )
-            w1.append(wp)
-            s1.append(sp)
 
         inv_us = sbuf("inv_us", [P, PACK - 1], F32)
         nc.vector.reciprocal(out=inv_us[:], in_=us_t[:, 0 : PACK - 1])
@@ -122,17 +121,17 @@ def tile_mix_hidden_over_its_peak_kernel(
                 stop=stop,
             )
 
+
         zb = [ps.tile([P, T], F32, name="z%d" % j, tag="bank%d" % j) for j in range(3)]
-        zl = [ps.tile([P, T // 2], F32, name="zl%d" % h, tag="bank%d" % (3 + h)) for h in range(2)]
-        for g in range(3):
-            for j in range(2):
-                z_pass(zb[j][:], j, g, 0, T, g == 0, g == 2)
-        for g in range(3):
-            z_pass(zb[2][:], 2, g, 0, T, g == 0, g == 2)
-        for h in range(2):
+        zl = [ps.tile([P, HALF], F32, name="zl%d" % h, tag="bank%d" % (3 + h)) for h in range(2)]
+
+        def z_whole(j, g):
+            z_pass(zb[j][:], j, g, 0, T, g == 0, g == 2)
+
+        def z_last(h):
             for g in range(3):
                 for c in range(2):
-                    z_pass(zl[h][:, CH * c : CH * (c + 1)], 3, g, 256 * h + CH * c, CH,
+                    z_pass(zl[h][:, CH * c : CH * (c + 1)], 3, g, HALF * h + CH * c, CH,
                            g == 0 and c == 0, g == 2 and c == 1)
 
         zs = sbuf("zs", [P, PACK, T], F32)
@@ -140,27 +139,43 @@ def tile_mix_hidden_over_its_peak_kernel(
         denom = sbuf("denom", [P, PACK], F32)
         part = sbuf("part", [P, 1], F32)
         gain = sbuf("gain", [P, PACK], F32)
-        mag = [sbuf("mag%d" % h, [P, T // 2], F32) for h in range(2)]
-        for j in range(3):
+        mag = [sbuf("mag%d" % h, [P, HALF], F32) for h in range(2)]
+
+        def whole_peak(j):
             nc.scalar.activation(out=zs[:, j, :], in_=zb[j][:], func=ACT.Copy)
             nc.vector.tensor_reduce(
                 out=peak[:, j : j + 1], in_=zs[:, j, :], axis=AXIS.X, op=ALU.max, apply_absolute_value=True
             )
-        for h in range(2):
+
+        def last_peak(h, so_far, result):
             nc.scalar.activation(out=mag[h][:], in_=zl[h][:], func=ACT.Abs)
+            nc.vector.tensor_scalar(
+                out=mag[h][:], in0=mag[h][:], scalar1=TENTH, scalar2=so_far, op0=ALU.add, op1=ALU.max,
+                accum_out=result,
+            )
+
+        z_whole(0, 0)
+        z_whole(0, 1)
+        z_whole(1, 0)
+        z_whole(0, 2)
+        z_whole(1, 1)
+        z_whole(1, 2)
+        z_last(0)
+        for g in range(3):
+            z_whole(2, g)
+        z_last(1)
+
+        whole_peak(0)
+        whole_peak(1)
+        last_peak(0, None, part[:])
+        whole_peak(2)
+        last_peak(1, part[:], denom[:, 3:4])
         for h in range(2):
             nc.scalar.activation(
-                out=zs[:, 3, 256 * h : 256 * (h + 1)], in_=zl[h][:], func=ACT.Copy, scale=us_t[:, 3:4]
+                out=zs[:, 3, HALF * h : HALF * (h + 1)], in_=zl[h][:], func=ACT.Copy, scale=us_t[:, 3:4]
             )
-        nc.vector.tensor_scalar(
-            out=mag[0][:], in0=mag[0][:], scalar1=TENTH, scalar2=None, op0=ALU.add, op1=ALU.max, accum_out=part[:]
-        )
         nc.vector.scalar_tensor_tensor(
             out=denom[:, 0:3], in0=peak[:], scalar=TENTH, in1=inv_us[:], op0=ALU.add, op1=ALU.mult
-        )
-        nc.vector.tensor_scalar(
-            out=mag[1][:], in0=mag[1][:], scalar1=TENTH, scalar2=part[:], op0=ALU.add, op1=ALU.max,
-            accum_out=denom[:, 3:4],
         )
         nc.vector.reciprocal(out=gain[:], in_=denom[:])
 
@@ -178,10 +193,19 @@ def tile_mix_hidden_over_its_peak_kernel(
                 op=ALU.mult,
             )
 
+        def scale_tokens_scalar(c, a, b):
+            for j in range(PACK):
+                nc.scalar.activation(
+                    out=hb[c][:].rearrange("p (t j) -> p j t", j=PACK)[:, j, a:b],
+                    in_=zs[:, j, CH * c + a : CH * c + b],
+                    func=ACT.Copy,
+                    scale=gain[:, j : j + 1],
+                )
+
         def quantize(c):
             nc.vector.quantize_mx(out=hq[c][:].bitcast(FP8X4), scales=hs[c][:], in_=hb[c][:])
 
-        banks = [(0, 0, 4, 5), (1, 0, 4, 6), (2, 0, 4, 7), (3, 0, 2, 0), (3, 2, 2, 1)]
+        banks = [(b // 2, 2 * (b % 2), 2, (5 + b) % 8) for b in range(8)]
         yb = {}
 
         def skip(b):
@@ -225,23 +249,26 @@ def tile_mix_hidden_over_its_peak_kernel(
                 nc.scalar.copy(out=res[:], in_=yb[b][:])
             nc.sync.dma_start(out=out_v[:, n0 : n0 + nn, CH * c : CH * (c + 1)], in_=res[:])
 
-        skip(0)
-        skip(1)
-        skip(2)
+        for b in range(len(banks)):
+            skip(b)
+
+        def finish(c, second_half_on_vector):
+            for h in range(2):
+                second(2 * c + h)
+                drain(2 * c + h, h == 1 and second_half_on_vector)
+
+        scale_tokens_scalar(2, 0, SCALAR_TOKENS)
         scale_tokens(0, 0, CH)
-        for c in range(chunks):
-            if c + 1 < chunks:
-                scale_tokens(c + 1, 0, CH // 2)
-            quantize(c)
-            if c + 1 < chunks:
-                scale_tokens(c + 1, CH // 2, CH)
-            if c < 3:
-                second(c)
-                drain(c, False)
-            if c == 0:
-                skip(3)
-                skip(4)
-        second(3)
-        second(4)
-        drain(3, False)
-        drain(4, True)
+        scale_tokens(1, 0, CH // 2)
+        quantize(0)
+        finish(0, False)
+        scale_tokens(1, CH // 2, CH)
+        scale_tokens(2, SCALAR_TOKENS, CH)
+        quantize(1)
+        finish(1, False)
+        scale_tokens(3, 0, CH // 2)
+        quantize(2)
+        scale_tokens(3, CH // 2, CH)
+        quantize(3)
+        finish(2, True)
+        finish(3, True)

@@ -67,16 +67,16 @@ def tile_mix_hidden_over_its_peak_kernel(
         wb_s = plane("wb_s", 1)
 
         queues = [nc.sync, nc.scalar]
-        wa_w = load_fp4(nc.sync, "wa_w", wa_words)
+        xq_w = load_fp8(nc.sync, "xq_w", xq_words)
         for r in range(4):
             load_scale_rows(queues[(r + 1) % 2], wa_s, wa_scales, r)
-        wc_w = load_fp4(nc.scalar, "wc_w", wc_words)
+        wa_w = load_fp4(nc.scalar, "wa_w", wa_words)
         load_scale_rows(nc.sync, wc_s, wc_scales, 0)
         xt_w = load_fp8(nc.scalar, "xt_w", xt_words)
         load_scale_rows(nc.gpsimd, wc_s, wc_scales, 3)
         for r in range(4):
             load_scale_rows(queues[r % 2], xt_s, xt_scales, r)
-        xq_w = load_fp8(nc.sync, "xq_w", xq_words)
+        wc_w = load_fp4(nc.sync, "wc_w", wc_words)
         for r in range(1, 3):
             load_scale_rows(queues[r % 2], wc_s, wc_scales, r)
         for r in range(4):
@@ -121,6 +121,17 @@ def tile_mix_hidden_over_its_peak_kernel(
                 stop=stop,
             )
 
+        warm = ps.tile([P, T], F32, name="warm", tag="bank7")
+        for i in range(3):
+            nc.tensor.matmul_mx(
+                out=warm[:],
+                lhsT=xq_w[:, 0, 0:P].bitcast(FP8X4),
+                lhsT_scale=wa_s[:, 0, 0:P],
+                rhs=xq_w[:, 0, :].bitcast(FP8X4),
+                rhs_scale=wa_s[:, 0, :],
+                start=True,
+                stop=True,
+            )
 
         zb = [ps.tile([P, T], F32, name="z%d" % j, tag="bank%d" % j) for j in range(3)]
         zl = [ps.tile([P, HALF], F32, name="zl%d" % h, tag="bank%d" % (3 + h)) for h in range(2)]
@@ -154,21 +165,19 @@ def tile_mix_hidden_over_its_peak_kernel(
                 accum_out=result,
             )
 
-        z_whole(0, 0)
-        z_whole(0, 1)
-        z_whole(1, 0)
-        z_whole(0, 2)
-        z_whole(1, 1)
-        z_whole(1, 2)
+        for j in range(2):
+            for g in range(2):
+                z_whole(j, g)
         z_last(0)
+        for j in range(2):
+            z_whole(j, 2)
         for g in range(3):
             z_whole(2, g)
         z_last(1)
 
-        whole_peak(0)
-        whole_peak(1)
         last_peak(0, None, part[:])
-        whole_peak(2)
+        for j in range(3):
+            whole_peak(j)
         last_peak(1, part[:], denom[:, 3:4])
         for h in range(2):
             nc.scalar.activation(
@@ -257,18 +266,16 @@ def tile_mix_hidden_over_its_peak_kernel(
                 second(2 * c + h)
                 drain(2 * c + h, h == 1 and second_half_on_vector)
 
-        scale_tokens_scalar(2, 0, SCALAR_TOKENS)
+        scale_tokens_scalar(1, 0, SCALAR_TOKENS)
         scale_tokens(0, 0, CH)
-        scale_tokens(1, 0, CH // 2)
+        scale_tokens(1, SCALAR_TOKENS, CH)
         quantize(0)
         finish(0, False)
-        scale_tokens(1, CH // 2, CH)
-        scale_tokens(2, SCALAR_TOKENS, CH)
+        scale_tokens(2, 0, CH)
         quantize(1)
         finish(1, False)
-        scale_tokens(3, 0, CH // 2)
         quantize(2)
-        scale_tokens(3, CH // 2, CH)
+        scale_tokens(3, 0, CH)
         quantize(3)
         finish(2, True)
         finish(3, True)

@@ -22,7 +22,7 @@ PACK = 4
 CH = 128
 HALF = T // 2
 TENTH = 0.1
-SCALAR_TOKENS = 96
+SCALAR_TOKENS = 80
 
 
 def tile_mix_hidden_over_its_peak_kernel(
@@ -72,13 +72,14 @@ def tile_mix_hidden_over_its_peak_kernel(
             load_scale_rows(queues[(r + 1) % 2], wa_s, wa_scales, r)
         wa_w = load_fp4(nc.scalar, "wa_w", wa_words)
         load_scale_rows(nc.sync, wc_s, wc_scales, 0)
-        xt_w = load_fp8(nc.scalar, "xt_w", xt_words)
+        xt_w = [load_fp8(nc.scalar, "xt_w0", xt_words[0:1])]
         load_scale_rows(nc.gpsimd, wc_s, wc_scales, 3)
         for r in range(4):
             load_scale_rows(queues[r % 2], xt_s, xt_scales, r)
-        wc_w = load_fp4(nc.sync, "wc_w", wc_words)
+        xt_w.append(load_fp8(nc.sync, "xt_w1", xt_words[1:2]))
+        wc_w = load_fp4(nc.scalar, "wc_w", wc_words)
         for r in range(1, 3):
-            load_scale_rows(queues[r % 2], wc_s, wc_scales, r)
+            load_scale_rows(queues[(r + 1) % 2], wc_s, wc_scales, r)
         for r in range(4):
             load_scale_rows(nc.sync, xq_s, xq_scales, r)
         us_t = sbuf("us_t", [P, PACK], F32)
@@ -91,8 +92,8 @@ def tile_mix_hidden_over_its_peak_kernel(
             load_scale_rows(nc.sync, wb_s, wb_scales, r)
 
         passes = [
-            (wa_w[:, 0, :], wa_s[:, 0, :], xt_w[:, 0, :], xt_s[:, 0, :]),
-            (wa_w[:, 1, :], wa_s[:, 1, :], xt_w[:, 1, :], xt_s[:, 1, :]),
+            (wa_w[:, 0, :], wa_s[:, 0, :], xt_w[0][:, 0, :], xt_s[:, 0, :]),
+            (wa_w[:, 1, :], wa_s[:, 1, :], xt_w[1][:, 0, :], xt_s[:, 1, :]),
             (wc_w[:, 0, :], wc_s[:, 0, :], xq_w[:, 0, :], xq_s[:, 0, :]),
         ]
         w1 = [sbuf("w1_%d" % g, [P, 1024], U8) for g in range(3)]
@@ -227,7 +228,7 @@ def tile_mix_hidden_over_its_peak_kernel(
                         out=yb[b][:, i, :],
                         lhsT=wy_w[:, g, 256 * n : 256 * (n + 1)].bitcast(FP4X4),
                         lhsT_scale=wy_s[:, g, P * n : P * (n + 1)],
-                        rhs=xt_w[:, g, CH * c : CH * (c + 1)].bitcast(FP8X4),
+                        rhs=xt_w[g][:, 0, CH * c : CH * (c + 1)].bitcast(FP8X4),
                         rhs_scale=xt_s[:, g, CH * c : CH * (c + 1)],
                         start=(i == 0 and g == 0),
                         stop=False,
@@ -256,9 +257,10 @@ def tile_mix_hidden_over_its_peak_kernel(
                 nc.vector.tensor_copy(out=res[:], in_=yb[b][:])
             else:
                 nc.scalar.copy(out=res[:], in_=yb[b][:])
-            nc.sync.dma_start(out=out_v[:, n0 : n0 + nn, CH * c : CH * (c + 1)], in_=res[:])
+            queue = nc.scalar if b == 6 else nc.sync
+            queue.dma_start(out=out_v[:, n0 : n0 + nn, CH * c : CH * (c + 1)], in_=res[:])
 
-        for b in range(len(banks)):
+        for b in range(6):
             skip(b)
 
         def finish(c, second_half_on_vector):
@@ -271,6 +273,8 @@ def tile_mix_hidden_over_its_peak_kernel(
         scale_tokens(1, SCALAR_TOKENS, CH)
         quantize(0)
         finish(0, False)
+        skip(6)
+        skip(7)
         scale_tokens(2, 0, CH)
         quantize(1)
         finish(1, False)

from contextlib import ExitStack

import concourse.mybir as mybir

K, L, T, R, N = 1024, 512, 512, 512, 512
FLOPS = 2 * T * (K * R + L * R + R * N + K * N)

F32 = mybir.dt.float32
BF16 = mybir.dt.bfloat16
I32 = mybir.dt.int32
U32 = mybir.dt.uint32
U16 = mybir.dt.uint16
U8 = mybir.dt.uint8
FP8X4 = mybir.dt.float8_e4m3fn_x4
FP4X4 = mybir.dt.float4_e2m1fn_x4
ALU = mybir.AluOpType
ACT = mybir.ActivationFunctionType
AXIS = mybir.AxisListType

P = 128
PACK = 4
CH = 128
HALF = T // 2
TENTH = 0.1
SCALAR_TOKENS = 80


def tile_mix_hidden_over_its_peak_kernel(
    tc, xt_words, xt_scales, wa_words, wa_scales, xq_words, xq_scales, wc_words, wc_scales,
    us, wb_words, wb_scales, wy_words, wy_scales, out,
):
    nc = tc.nc
    with ExitStack() as ctx:
        sb = ctx.enter_context(tc.tile_pool(name="sb", bufs=1))
        ps = ctx.enter_context(tc.psum_pool(name="ps", bufs=1))
        ctx.enter_context(tc.manual_schedule())

        def sbuf(name, shape, dtype):
            return sb.tile(shape, dtype, name=name, align_bytes=64)

        def plane(name, passes):
            t = sbuf(name, [P, passes, 512], U8)
            nc.vector.memset(t[:].bitcast(I32), 0)
            return t

        def load_scale_rows(queue, dst, src, r):
            queue.dma_start(
                out=dst[r:P:32, :, :].bitcast(I32),
                in_=src.rearrange("g (q r) c -> r q g c", r=4)[r].bitcast(I32),
            )

        def load_fp8(queue, name, src):
            t = sbuf(name, [P, src.shape[0], 512], U32)
            queue.dma_start(out=t[:].bitcast(I32), in_=src.rearrange("g p n t -> p g (n t)").bitcast(I32))
            return t

        def load_fp4(queue, name, src):
            t = sbuf(name, [P, src.shape[0], 1024], U8)
            queue.dma_start(out=t[:].bitcast(I32), in_=src.rearrange("g p b -> p g b").bitcast(I32))
            return t

        wa_s = plane("wa_s", 2)
        wc_s = plane("wc_s", 1)
        xt_s = plane("xt_s", 2)
        xq_s = plane("xq_s", 1)
        wy_s = plane("wy_s", 2)
        wb_s = plane("wb_s", 1)

        queues = [nc.sync, nc.scalar]
        xq_w = load_fp8(nc.sync, "xq_w", xq_words)
        for r in range(4):
            load_scale_rows(queues[(r + 1) % 2], wa_s, wa_scales, r)
        wa_w = load_fp4(nc.scalar, "wa_w", wa_words)
        load_scale_rows(nc.sync, wc_s, wc_scales, 0)
        xt_w = [load_fp8(nc.scalar, "xt_w0", xt_words[0:1])]
        load_scale_rows(nc.gpsimd, wc_s, wc_scales, 3)
        for r in range(4):
            load_scale_rows(queues[r % 2], xt_s, xt_scales, r)
        xt_w.append(load_fp8(nc.sync, "xt_w1", xt_words[1:2]))
        wc_w = load_fp4(nc.scalar, "wc_w", wc_words)
        for r in range(1, 3):
            load_scale_rows(queues[(r + 1) % 2], wc_s, wc_scales, r)
        for r in range(4):
            load_scale_rows(nc.sync, xq_s, xq_scales, r)
        us_t = sbuf("us_t", [P, PACK], F32)
        nc.sync.dma_start(out=us_t[:], in_=us.rearrange("(p j) o -> p (j o)", j=PACK))
        wy_w = load_fp4(nc.sync, "wy_w", wy_words)
        for r in range(4):
            load_scale_rows(nc.sync, wy_s, wy_scales, r)
        wb_w = load_fp8(nc.sync, "wb_w", wb_words)
        for r in range(4):
            load_scale_rows(nc.sync, wb_s, wb_scales, r)

        passes = [
            (wa_w[:, 0, :], wa_s[:, 0, :], xt_w[0][:, 0, :], xt_s[:, 0, :]),
            (wa_w[:, 1, :], wa_s[:, 1, :], xt_w[1][:, 0, :], xt_s[:, 1, :]),
            (wc_w[:, 0, :], wc_s[:, 0, :], xq_w[:, 0, :], xq_s[:, 0, :]),
        ]
        w1 = [sbuf("w1_%d" % g, [P, 1024], U8) for g in range(3)]
        s1 = [sbuf("s1_%d" % g, [P, 512], U8) for g in range(3)]
        for g in range(3):
            nc.vector.tensor_copy(
                out=w1[g][:].bitcast(U16).rearrange("p (j m) -> p j m", j=PACK),
                in_=passes[g][0].bitcast(U16).rearrange("p (m j) -> p j m", j=PACK),
            )
            nc.vector.tensor_copy(
                out=s1[g][:].rearrange("p (j m) -> p j m", j=PACK),
                in_=passes[g][1].rearrange("p (m j) -> p j m", j=PACK),
            )

        inv_us = sbuf("inv_us", [P, PACK - 1], F32)
        nc.vector.reciprocal(out=inv_us[:], in_=us_t[:, 0 : PACK - 1])

        def z_pass(dst, j, g, t0, width, start, stop):
            nc.tensor.matmul_mx(
                out=dst,
                lhsT=w1[g][:, 256 * j : 256 * (j + 1)].bitcast(FP4X4),
                lhsT_scale=s1[g][:, P * j : P * (j + 1)],
                rhs=passes[g][2][:, t0 : t0 + width].bitcast(FP8X4),
                rhs_scale=passes[g][3][:, t0 : t0 + width],
                start=start,
                stop=stop,
            )

        warm = ps.tile([P, T], F32, name="warm", tag="bank7")
        for i in range(3):
            nc.tensor.matmul_mx(
                out=warm[:],
                lhsT=xq_w[:, 0, 0:P].bitcast(FP8X4),
                lhsT_scale=wa_s[:, 0, 0:P],
                rhs=xq_w[:, 0, :].bitcast(FP8X4),
                rhs_scale=wa_s[:, 0, :],
                start=True,
                stop=True,
            )

        zb = [ps.tile([P, T], F32, name="z%d" % j, tag="bank%d" % j) for j in range(3)]
        zl = [ps.tile([P, HALF], F32, name="zl%d" % h, tag="bank%d" % (3 + h)) for h in range(2)]

        def z_whole(j, g):
            z_pass(zb[j][:], j, g, 0, T, g == 0, g == 2)

        def z_last(h):
            for g in range(3):
                for c in range(2):
                    z_pass(zl[h][:, CH * c : CH * (c + 1)], 3, g, HALF * h + CH * c, CH,
                           g == 0 and c == 0, g == 2 and c == 1)

        zs = sbuf("zs", [P, PACK, T], F32)
        peak = sbuf("peak", [P, PACK - 1], F32)
        denom = sbuf("denom", [P, PACK], F32)
        part = sbuf("part", [P, 1], F32)
        gain = sbuf("gain", [P, PACK], F32)
        mag = [sbuf("mag%d" % h, [P, HALF], F32) for h in range(2)]

        def whole_peak(j):
            nc.scalar.activation(out=zs[:, j, :], in_=zb[j][:], func=ACT.Copy)
            nc.vector.tensor_reduce(
                out=peak[:, j : j + 1], in_=zs[:, j, :], axis=AXIS.X, op=ALU.max, apply_absolute_value=True
            )

        def last_peak(h, so_far, result):
            nc.scalar.activation(out=mag[h][:], in_=zl[h][:], func=ACT.Abs)
            nc.vector.tensor_scalar(
                out=mag[h][:], in0=mag[h][:], scalar1=TENTH, scalar2=so_far, op0=ALU.add, op1=ALU.max,
                accum_out=result,
            )

        for j in range(2):
            for g in range(2):
                z_whole(j, g)
        z_last(0)
        for j in range(2):
            z_whole(j, 2)
        for g in range(3):
            z_whole(2, g)
        z_last(1)

        last_peak(0, None, part[:])
        for j in range(3):
            whole_peak(j)
        last_peak(1, part[:], denom[:, 3:4])
        for h in range(2):
            nc.scalar.activation(
                out=zs[:, 3, HALF * h : HALF * (h + 1)], in_=zl[h][:], func=ACT.Copy, scale=us_t[:, 3:4]
            )
        nc.vector.scalar_tensor_tensor(
            out=denom[:, 0:3], in0=peak[:], scalar=TENTH, in1=inv_us[:], op0=ALU.add, op1=ALU.mult
        )
        nc.vector.reciprocal(out=gain[:], in_=denom[:])

        chunks = T // CH
        hb = [sbuf("hb%d" % c, [P, CH * PACK], BF16) for c in range(chunks)]
        hq = [sbuf("hq%d" % c, [P, CH], U32) for c in range(chunks)]
        hs = [sbuf("hs%d" % c, [P, CH], U8) for c in range(chunks)]

        def scale_tokens(c, a, b):
            u = (b - a) // 2
            nc.vector.tensor_tensor(
                out=hb[c][:, PACK * a : PACK * b].rearrange("p (u i j) -> p u j i", i=2, j=PACK),
                in0=zs[:, :, CH * c + a : CH * c + b].rearrange("p j (u i) -> p u j i", i=2),
                in1=gain[:].rearrange("p (a j b) -> p a j b", a=1, b=1).broadcast_to([P, u, PACK, 2]),
                op=ALU.mult,
            )

        def scale_tokens_scalar(c, a, b):
            for j in range(PACK):
                nc.scalar.activation(
                    out=hb[c][:].rearrange("p (t j) -> p j t", j=PACK)[:, j, a:b],
                    in_=zs[:, j, CH * c + a : CH * c + b],
                    func=ACT.Copy,
                    scale=gain[:, j : j + 1],
                )

        def quantize(c):
            nc.vector.quantize_mx(out=hq[c][:].bitcast(FP8X4), scales=hs[c][:], in_=hb[c][:])

        banks = [(b // 2, 2 * (b % 2), 2, (5 + b) % 8) for b in range(8)]
        yb = {}

        def skip(b):
            c, n0, nn, bank = banks[b]
            yb[b] = ps.tile([P, nn, CH], F32, name="y%d" % b, tag="bank%d" % bank)
            for i in range(nn):
                for g in range(2):
                    n = n0 + i
                    nc.tensor.matmul_mx(
                        out=yb[b][:, i, :],
                        lhsT=wy_w[:, g, 256 * n : 256 * (n + 1)].bitcast(FP4X4),
                        lhsT_scale=wy_s[:, g, P * n : P * (n + 1)],
                        rhs=xt_w[g][:, 0, CH * c : CH * (c + 1)].bitcast(FP8X4),
                        rhs_scale=xt_s[:, g, CH * c : CH * (c + 1)],
                        start=(i == 0 and g == 0),
                        stop=False,
                    )

        def second(b):
            c, n0, nn, bank = banks[b]
            for i in range(nn):
                n = n0 + i
                nc.tensor.matmul_mx(
                    out=yb[b][:, i, :],
                    lhsT=wb_w[:, 0, P * n : P * (n + 1)].bitcast(FP8X4),
                    lhsT_scale=wb_s[:, 0, P * n : P * (n + 1)],
                    rhs=hq[c][:].bitcast(FP8X4),
                    rhs_scale=hs[c][:],
                    start=False,
                    stop=(i == nn - 1),
                )

        out_v = out.rearrange("(i p) t -> p i t", p=P)

        def drain(b, on_vector):
            c, n0, nn, bank = banks[b]
            res = sbuf("res%d" % b, [P, nn, CH], F32)
            if on_vector:
                nc.vector.tensor_copy(out=res[:], in_=yb[b][:])
            else:
                nc.scalar.copy(out=res[:], in_=yb[b][:])
            queue = nc.scalar if b == 6 else nc.sync
            queue.dma_start(out=out_v[:, n0 : n0 + nn, CH * c : CH * (c + 1)], in_=res[:])

        for b in range(6):
            skip(b)

        def finish(c, second_half_on_vector):
            for h in range(2):
                second(2 * c + h)
                drain(2 * c + h, h == 1 and second_half_on_vector)

        scale_tokens_scalar(1, 0, SCALAR_TOKENS)
        scale_tokens(0, 0, CH)
        scale_tokens(1, SCALAR_TOKENS, CH)
        quantize(0)
        finish(0, False)
        skip(6)
        skip(7)
        scale_tokens(2, 0, CH)
        quantize(1)
        finish(1, False)
        quantize(2)
        scale_tokens(3, 0, CH)
        quantize(3)
        finish(2, True)
        finish(3, True)
